import numpy as np
import ml_dtypes


def mxq(x, axis, fmt="e4m3"):
    dtype, down = {"e4m3": (ml_dtypes.float8_e4m3fn, 7), "e5m2": (ml_dtypes.float8_e5m2, 14)}[fmt]
    v = np.moveaxis(np.asarray(x, np.float32).astype(ml_dtypes.bfloat16).astype(np.float64), axis, -1)
    blocks = v.reshape(v.shape[:-1] + (-1, 32))
    amax = np.abs(blocks).max(-1, keepdims=True)
    byte = np.maximum(np.where(amax > 0, np.frexp(amax)[1] - 1 + 127, 0) - down, 1)
    scale = np.exp2(byte - 127.0)
    codes = (blocks / scale).astype(np.float32).astype(dtype).astype(np.float64)
    return np.moveaxis((codes * scale).reshape(v.shape), -1, axis)


WIDE = False


def mx_kscale(k):
    if not WIDE:
        return np.ones(k)
    levels = np.array([10, -10, 5, -5, 0])
    if k % 512:
        return np.exp2(np.random.permutation(np.resize(levels, k // 32))).repeat(32)
    a = np.empty((k // 512, 16))
    for p in range(k // 512):
        a[p, :8] = np.random.permutation(np.resize(levels, 8))
        for g in range(8):
            far = levels[np.abs(levels - a[p, g]) >= 10]
            a[p, g + 8] = far[np.random.randint(len(far))]
    return np.exp2(a.ravel()).repeat(32)


def f64(x):
    return np.asarray(x).astype(np.float64)


def striped(idx):
    return np.tile(idx.reshape(-1, 16).T, (8, 1)).astype(np.uint16)


def unstriped(offs):
    return offs[:16].T.reshape(-1).astype(np.int64)


def striped8(idx):
    return np.concatenate([x.reshape(-1, 16).T for x in idx]).astype(np.uint16)


def runs(offs, k):
    lists = np.stack([offs[16 * r : 16 * r + 16].T.reshape(-1) for r in range(8)]).astype(np.int64)
    return lists[np.arange(k) % 512 // 64]


def pack_weight(w):
    k, n = w.shape
    w = f64(np.asarray(w, np.float32).astype(ml_dtypes.bfloat16)).reshape(k // 32, 32, n)
    amax = np.abs(w).max(1)
    byte = np.clip(np.where(amax > 0, np.frexp(amax)[1] - 1 + 127 - 7, 1), 1, 254)
    scaled = (w * np.exp2(127.0 - byte)[:, None, :]).reshape(k, n).astype(np.float32)
    words = np.ascontiguousarray(scaled.reshape(k // 512, 128, 4, n).transpose(0, 1, 3, 2)).astype(ml_dtypes.float8_e4m3fn).view(np.uint8)
    return words, np.ascontiguousarray(byte.astype(np.uint8).reshape(k // 512, 16, n))


def unpack_weight(words, scales):
    g, p, n, _ = words.shape
    vals = np.ascontiguousarray(words).view(ml_dtypes.float8_e4m3fn).astype(np.float64) * np.repeat(np.exp2(scales.astype(np.float64) - 127.0), 8, axis=1)[..., None]
    return vals.transpose(0, 1, 3, 2).reshape(g * 512, n)


def sigmoid(v):
    return 1.0 / (1.0 + np.exp(-np.maximum(v, -700.0)))

def planes(y):
    n, m = y.shape
    v = y.astype(np.float32).astype(ml_dtypes.bfloat16).astype(np.float64).reshape(n // 32, 32, m)
    top = np.abs(v).max(1)
    byte = np.clip(np.where(top > 0, np.frexp(top)[1] - 1 + 127 - 7, 1), 1, 254)
    codes = (v * np.exp2(127.0 - byte)[:, None, :]).reshape(n, m).astype(np.float32).astype(ml_dtypes.float8_e4m3fn).view(np.uint8)
    words = codes.reshape(n // 512, 128, 4, m).transpose(0, 1, 3, 2)
    return np.ascontiguousarray(words), np.ascontiguousarray(byte.astype(np.uint8).reshape(n // 512, 16, m))


K, T, S, N, H, J = 512, 2048, 256, 512, 512, 512


def setup_inputs():
    n = np.random.standard_normal
    s = mx_kscale(K)[:, None]
    u = mx_kscale(H)
    packed_xT = pack_weight(n((K, T)) * s)
    packed_w1 = pack_weight(n((K, H)) / np.sqrt(K) / s)
    packed_w2 = pack_weight(n((H, N)) / np.sqrt(2 * H) / u[:, None])
    packed_w3 = pack_weight(n((H, N)) / np.sqrt(2 * H) / u[:, None])
    return {
        "x_words": packed_xT[0],
        "x_scales": packed_xT[1],
        "w1_words": packed_w1[0],
        "w1_scales": packed_w1[1],
        "gn": (np.random.uniform(0.5, 1.5, (H, 1)) * u[:, None]).astype(np.float32),
        "gm": (np.random.uniform(0.5, 1.5, (H, 1)) * u[:, None]).astype(np.float32),
        "w2_words": packed_w2[0],
        "w2_scales": packed_w2[1],
        "w3_words": packed_w3[0],
        "w3_scales": packed_w3[1],
        "offs": striped(np.random.permutation(T)[:S]),
        "n1": striped(np.random.randint(0, S, J)),
        "n2": striped8(np.stack([np.random.permutation(S) for _ in range(8)])),
        "n3": striped8(np.stack([np.random.permutation(S) for _ in range(8)])),
        "n4": striped8(np.stack([np.random.permutation(S) for _ in range(8)])),
        "n5": striped8(np.stack([np.random.permutation(S) for _ in range(8)])),
    }


def reference(x_words, x_scales, w1_words, w1_scales, gn, gm, w2_words, w2_scales, w3_words, w3_scales, offs, n1, n2, n3, n4, n5):
    xq = unpack_weight(x_words, x_scales)[:, unstriped(offs)]
    y = unpack_weight(w1_words, w1_scales).T @ xq
    mb = y[:, unstriped(n1)]
    ms = mb.reshape(H, S, 2).sum(axis=2)
    mx = mb.reshape(H, S, 2).max(axis=2)
    z = f64(gn) * (ms - np.maximum(y, mx))
    z2 = f64(gm) * (y + y[np.arange(H)[:, None], runs(n2, H)] - (np.maximum(y[np.arange(H)[:, None], runs(n3, H)], y[np.arange(H)[:, None], runs(n4, H)])))
    h = unpack_weight(w2_words, w2_scales).T @ mxq(z, 0, "e4m3") + unpack_weight(w3_words, w3_scales).T @ mxq(z2, 0, "e4m3")
    out_0 = h * (sigmoid(h[np.arange(N)[:, None], runs(n5, N)]))
    return (out_0,) + planes(out_0)

@@ -1,0 +1,218 @@
+from contextlib import ExitStack
+
+import concourse.mybir as mybir
+
+F32 = mybir.dt.float32
+BF16 = mybir.dt.bfloat16
+I32 = mybir.dt.int32
+U32 = mybir.dt.uint32
+U16 = mybir.dt.uint16
+U8 = mybir.dt.uint8
+FP8X4 = mybir.dt.float8_e4m3fn_x4
+ALU = mybir.AluOpType
+ACT = mybir.ActivationFunctionType
+
+P = 128
+PACK = 4
+T = 2048
+S = 256
+H = 512
+HALF = S // 2
+WINDOW = 2 * S
+RUN = 4
+FLOPS = 3 * 2 * 512 * 512 * 256
+
+
+def words_of(dram):
+    return dram[0].rearrange("p n t -> p (n t)").bitcast(I32)
+
+
+def woven(ap):
+    return ap.rearrange("p (c i t) -> p c t i", i=RUN, t=PACK)
+
+
+def planes(ap):
+    return ap.rearrange("p t (c i) -> p c t i", i=RUN)
+
+
+def tile_picked_joingpairtrimgate_none_po_kernel(
+    tc, x_words, x_scales, w1_words, w1_scales, gn, gm, w2_words, w2_scales, w3_words, w3_scales,
+    offs, n1, n2, n3, n4, n5, out_0, out_1, out_2,
+):
+    nc = tc.nc
+    with ExitStack() as ctx:
+        lists = ctx.enter_context(tc.tile_pool(name="lists", bufs=1))
+        sb = ctx.enter_context(tc.tile_pool(name="sb", bufs=1))
+        psum = ctx.enter_context(tc.psum_pool(name="psum", bufs=1))
+
+        def tile(name, shape, dtype):
+            return sb.tile(shape, dtype, name=name, align_bytes=64)
+
+        def load_list(name, dram):
+            held = lists.tile(list(dram.shape), U16, name=name)
+            nc.sync.dma_start(held[:], dram)
+            return held
+
+        def load_scale_rows(queue, plane, first, dram, q):
+            queue.dma_start(
+                plane[32 * q + first : 32 * q + first + 4, :].bitcast(I32),
+                dram[0, 4 * q : 4 * q + 4, :].bitcast(I32),
+            )
+
+        def deal(dst, src, first=0, last=PACK):
+            nc.vector.tensor_copy(
+                dst.rearrange("p t m -> p m t"), src.rearrange("p (m t) -> p m t", t=PACK)[:, :, first:last]
+            )
+
+        xs = tile("xs", [P, T], U8)
+        w1s = tile("w1s", [P, H], U8)
+        w23s = tile("w23s", [P, H], U8)
+        nc.vector.memset(xs[:].bitcast(I32), 0)
+        nc.vector.memset(w1s[:].bitcast(I32), 0)
+        nc.vector.memset(w23s[:].bitcast(I32), 0)
+        window = [tile("window%d" % t, [P, WINDOW], F32) for t in range(PACK)]
+        for t in range(PACK):
+            nc.vector.memset(window[t][:, S:], 0.0)
+
+        offs_t = load_list("offs_t", offs)
+        n1_t = load_list("n1_t", n1)
+        gm_t = tile("gm_t", [P, PACK], F32)
+        nc.sync.dma_start(gm_t[:], gm.rearrange("(p t) o -> p (t o)", t=PACK))
+        for q in range(4):
+            load_scale_rows(nc.scalar, xs, 0, x_scales, q)
+        for q in range(4):
+            load_scale_rows(nc.scalar if q < 3 else nc.gpsimd, w1s, 0, w1_scales, q)
+        xw = tile("xw", [P, T], U32)
+        nc.sync.dma_start(xw[:].bitcast(I32), words_of(x_words))
+        w1w = tile("w1w", [P, H], U32)
+        nc.sync.dma_start(w1w[:].bitcast(I32), words_of(w1_words))
+        n3_t = load_list("n3_t", n3)
+        n4_t = load_list("n4_t", n4)
+        gn_t = tile("gn_t", [P, PACK], F32)
+        nc.sync.dma_start(gn_t[:], gn.rearrange("(p t) o -> p (t o)", t=PACK))
+        w2w = tile("w2w", [P, H], U32)
+        nc.sync.dma_start(w2w[:].bitcast(I32), words_of(w2_words))
+        w3w = tile("w3w", [P, H], U32)
+        nc.sync.dma_start(w3w[:].bitcast(I32), words_of(w3_words))
+        n2_t = load_list("n2_t", n2)
+        n5_t = load_list("n5_t", n5)
+        for first, dram in ((0, w2_scales), (4, w3_scales)):
+            for q in range(4):
+                load_scale_rows(nc.gpsimd, w23s, first, dram, q)
+
+        xgs = tile("xgs", [P, S], U8)
+        nc.vector.tensor_copy(xgs[:], xs[:].indirect(offs_t[:]))
+        xg = tile("xg", [P, S], U32)
+        nc.vector.tensor_copy(xg[:], xw[:].indirect(offs_t[:]))
+        w1d, w1sd = [], []
+        for first, last in ((0, 1), (1, PACK)):
+            dealt_scales = tile("w1sd%d" % first, [P, last - first, P], U8)
+            deal(dealt_scales[:], w1s[:], first, last)
+            dealt_words = tile("w1d%d" % first, [P, last - first, P], U32)
+            deal(dealt_words[:], w1w[:], first, last)
+            w1sd.extend(dealt_scales[:, t, :] for t in range(last - first))
+            w1d.extend(dealt_words[:, t, :] for t in range(last - first))
+
+        for t in range(PACK):
+            y_ps = psum.tile([P, S], F32, name="y_ps%d" % t)
+            nc.tensor.matmul_mx(
+                y_ps[:], lhsT=w1d[t].bitcast(FP8X4), lhsT_scale=w1sd[t],
+                rhs=xg[:].bitcast(FP8X4), rhs_scale=xgs[:], start=True, stop=True,
+            )
+            nc.vector.tensor_copy(window[t][:, :S], y_ps[:])
+
+        mb = [tile("mb%d" % t, [P, 2 * S], F32) for t in range(PACK)]
+        for t in range(PACK):
+            for u in range(2):
+                nc.scalar.activation(
+                    mb[t][:, u * S : (u + 1) * S], window[t][:].indirect(n1_t[:, 16 * u : 16 * u + 16]), ACT.Copy
+                )
+        y3 = [tile("y3_%d" % t, [P, S], F32) for t in range(PACK)]
+        y4 = [tile("y4_%d" % t, [P, S], F32) for t in range(PACK)]
+        for t in range(PACK):
+            nc.scalar.activation(y3[t][:], window[t][:].indirect(n3_t[:]), ACT.Copy)
+            nc.scalar.activation(y4[t][:], window[t][:].indirect(n4_t[:]), ACT.Copy)
+
+        yg = [tile("yg%d" % t, [P, S], F32) for t in range(PACK)]
+        for t in range(PACK):
+            nc.vector.tensor_scalar(yg[t][:], window[t][:, :S], gm_t[:, t : t + 1], None, ALU.mult)
+        yg2 = [tile("yg2_%d" % u, [P, PACK, HALF], F32) for u in range(2)]
+        for u in range(2):
+            for t in range(PACK):
+                nc.scalar.activation(yg2[u][:, t, :], yg[t][:].indirect(n2_t[:, 8 * u : 8 * u + 8]), ACT.Copy)
+
+        w2d = tile("w2d", [P, PACK, P], U32)
+        deal(w2d[:], w2w[:])
+        w3d = tile("w3d", [P, PACK, P], U32)
+        deal(w3d[:], w3w[:])
+        w23sd = tile("w23sd", [P, PACK, P], U8)
+        deal(w23sd[:], w23s[:])
+
+        top = [tile("top%d" % t, [P, S], F32) for t in range(PACK)]
+        gap = [tile("gap%d" % t, [P, S], F32) for t in range(PACK)]
+        trimmed = tile("trimmed", [P, PACK, S], F32)
+        for pair in ((0, 1), (2, 3)):
+            for t in pair:
+                nc.vector.tensor_tensor(top[t][:], mb[t][:, 0::2], window[t][:, :S], ALU.max)
+            for t in pair:
+                nc.vector.tensor_tensor(gap[t][:], mb[t][:, 1::2], top[t][:], ALU.subtract)
+            for t in pair:
+                nc.vector.scalar_tensor_tensor(trimmed[:, t, :], gap[t][:], 0.0, mb[t][:, 0::2], ALU.min, ALU.add)
+        z_bf = tile("z_bf", [P, S * PACK], BF16)
+        gn_wide = gn_t[:].rearrange("p (c t i) -> p c t i", c=1, i=1).to_broadcast([P, S // RUN, PACK, RUN])
+        nc.vector.tensor_tensor(woven(z_bf[:]), planes(trimmed[:]), gn_wide, ALU.mult)
+
+        top34 = [tile("top34_%d" % t, [P, S], F32) for t in range(PACK)]
+        rest = tile("rest", [P, PACK, S], F32)
+        zq = tile("zq", [P, S], U32)
+        zs = tile("zs", [P, S], U8)
+        for pair in ((0, 1), (2, 3)):
+            for t in pair:
+                nc.vector.tensor_tensor(top34[t][:], y3[t][:], y4[t][:], ALU.max)
+            if pair[0] == 0:
+                nc.vector.quantize_mx(zq[:].bitcast(FP8X4), zs[:], z_bf[:])
+            for t in pair:
+                nc.vector.scalar_tensor_tensor(
+                    rest[:, t, :], top34[t][:], gm_t[:, t : t + 1], yg[t][:], ALU.mult, ALU.subtract
+                )
+
+        h_ps = [psum.tile([P, S], F32, name="h_ps%d" % t) for t in range(PACK)]
+        for t in range(PACK):
+            nc.tensor.matmul_mx(
+                h_ps[t][:], lhsT=w2d[:, t, :].bitcast(FP8X4), lhsT_scale=w23sd[:, t, :],
+                rhs=zq[:].bitcast(FP8X4), rhs_scale=zs[:], start=True, stop=False,
+            )
+        for u in range(2):
+            cols = slice(u * HALF, (u + 1) * HALF)
+            z2_bf = tile("z2_bf%d" % u, [P, HALF * PACK], BF16)
+            nc.vector.tensor_tensor(woven(z2_bf[:]), planes(yg2[u][:]), planes(rest[:, :, cols]), ALU.subtract)
+            z2q = tile("z2q%d" % u, [P, HALF], U32)
+            z2s = tile("z2s%d" % u, [P, HALF], U8)
+            nc.vector.quantize_mx(z2q[:].bitcast(FP8X4), z2s[:], z2_bf[:])
+            for t in range(PACK):
+                nc.tensor.matmul_mx(
+                    h_ps[t][:, cols], lhsT=w3d[:, t, :].bitcast(FP8X4), lhsT_scale=w23sd[4:, t, :],
+                    rhs=z2q[:].bitcast(FP8X4), rhs_scale=z2s[:], start=False, stop=(u == 1),
+                )
+
+        for t in range(PACK):
+            nc.vector.tensor_copy(window[t][:, :S], h_ps[t][:])
+
+        oq = tile("oq", [P, S], U32)
+        osc = tile("osc", [P, S], U8)
+        out_rows = out_0.rearrange("(p t) j -> p t j", t=PACK)
+        for u in range(2):
+            cols = slice(u * HALF, (u + 1) * HALF)
+            gate = tile("gate%d" % u, [P, PACK, HALF], F32)
+            res = tile("res%d" % u, [P, PACK, HALF], F32)
+            for t in range(PACK):
+                nc.scalar.activation(gate[:, t, :], window[t][:].indirect(n5_t[:, 8 * u : 8 * u + 8]), ACT.Sigmoid)
+                nc.vector.tensor_tensor(res[:, t, :], gate[:, t, :], window[t][:, cols], ALU.mult)
+            nc.sync.dma_start(out_rows[:, :, cols], res[:])
+            res_bf = tile("res_bf%d" % u, [P, HALF * PACK], BF16)
+            nc.vector.tensor_copy(woven(res_bf[:]), planes(res[:]))
+            nc.vector.quantize_mx(oq[:, cols].bitcast(FP8X4), osc[:, cols], res_bf[:])
+            nc.sync.dma_start(words_of(out_1)[:, cols], oq[:, cols].bitcast(I32))
+        for q in range(4):
+            queue = nc.scalar if q % 2 else nc.sync
+            queue.dma_start(out_2[0, 4 * q : 4 * q + 4, :].bitcast(I32), osc[32 * q : 32 * q + 4, :].bitcast(I32))

@@ -19,7 +19,8 @@ S = 256
 H = 512
 HALF = S // 2
 WINDOW = 2 * S
-RUN = 4
+Y_WINDOW = 2 * S + 16
+RUN = 2
 FLOPS = 3 * 2 * 512 * 512 * 256
 
 
@@ -70,63 +71,62 @@ def tile_picked_joingpairtrimgate_none_po_kernel(
         nc.vector.memset(xs[:].bitcast(I32), 0)
         nc.vector.memset(w1s[:].bitcast(I32), 0)
         nc.vector.memset(w23s[:].bitcast(I32), 0)
-        window = [tile("window%d" % t, [P, WINDOW], F32) for t in range(PACK)]
-        for t in range(PACK):
-            nc.vector.memset(window[t][:, S:], 0.0)
+        window = [tile("window%d" % t, [P, Y_WINDOW], F32) for t in range(PACK)]
+        h_window = [tile("h_window%d" % t, [P, WINDOW], F32) for t in range(PACK)]
+        for held in window + h_window:
+            nc.vector.memset(held[:, S:], 0.0)
 
         offs_t = load_list("offs_t", offs)
         n1_t = load_list("n1_t", n1)
-        gm_t = tile("gm_t", [P, PACK], F32)
-        nc.sync.dma_start(gm_t[:], gm.rearrange("(p t) o -> p (t o)", t=PACK))
-        for q in range(4):
-            load_scale_rows(nc.scalar, xs, 0, x_scales, q)
-        for q in range(4):
-            load_scale_rows(nc.scalar if q < 3 else nc.gpsimd, w1s, 0, w1_scales, q)
-        xw = tile("xw", [P, T], U32)
-        nc.sync.dma_start(xw[:].bitcast(I32), words_of(x_words))
         w1w = tile("w1w", [P, H], U32)
         nc.sync.dma_start(w1w[:].bitcast(I32), words_of(w1_words))
-        n3_t = load_list("n3_t", n3)
-        n4_t = load_list("n4_t", n4)
-        gn_t = tile("gn_t", [P, PACK], F32)
-        nc.sync.dma_start(gn_t[:], gn.rearrange("(p t) o -> p (t o)", t=PACK))
+        for q in range(4):
+            load_scale_rows(nc.sync if q < 2 else nc.scalar, xs, 0, x_scales, q)
+        warm = tile("warm", [P, 1], F32)
+        nc.scalar.activation(warm[:], window[0][:, S : S + 1], ACT.Sigmoid)
+        xw = tile("xw", [P, T], U32)
+        nc.sync.dma_start(xw[:].bitcast(I32), words_of(x_words))
+        for q in range(4):
+            load_scale_rows(nc.sync, w1s, 0, w1_scales, q)
         w2w = tile("w2w", [P, H], U32)
         nc.sync.dma_start(w2w[:].bitcast(I32), words_of(w2_words))
         w3w = tile("w3w", [P, H], U32)
         nc.sync.dma_start(w3w[:].bitcast(I32), words_of(w3_words))
-        n2_t = load_list("n2_t", n2)
-        n5_t = load_list("n5_t", n5)
         for first, dram in ((0, w2_scales), (4, w3_scales)):
             for q in range(4):
-                load_scale_rows(nc.gpsimd, w23s, first, dram, q)
+                load_scale_rows(nc.sync, w23s, first, dram, q)
+        gm_t = tile("gm_t", [P, PACK], F32)
+        nc.gpsimd.dma_start(gm_t[:], gm.rearrange("(p t) o -> p (t o)", t=PACK))
+        gn_t = tile("gn_t", [P, PACK], F32)
+        nc.gpsimd.dma_start(gn_t[:], gn.rearrange("(p t) o -> p (t o)", t=PACK))
+        n3_t = load_list("n3_t", n3)
+        n4_t = load_list("n4_t", n4)
+        n2_t = load_list("n2_t", n2)
+        n5_t = load_list("n5_t", n5)
 
+        w1d = tile("w1d", [P, PACK, P], U32)
+        deal(w1d[:], w1w[:])
         xgs = tile("xgs", [P, S], U8)
         nc.vector.tensor_copy(xgs[:], xs[:].indirect(offs_t[:]))
         xg = tile("xg", [P, S], U32)
         nc.vector.tensor_copy(xg[:], xw[:].indirect(offs_t[:]))
-        w1d, w1sd = [], []
+        w1sd = []
         for first, last in ((0, 1), (1, PACK)):
             dealt_scales = tile("w1sd%d" % first, [P, last - first, P], U8)
             deal(dealt_scales[:], w1s[:], first, last)
-            dealt_words = tile("w1d%d" % first, [P, last - first, P], U32)
-            deal(dealt_words[:], w1w[:], first, last)
             w1sd.extend(dealt_scales[:, t, :] for t in range(last - first))
-            w1d.extend(dealt_words[:, t, :] for t in range(last - first))
 
         for t in range(PACK):
-            y_ps = psum.tile([P, S], F32, name="y_ps%d" % t)
+            y_ps = psum.tile([P, S], F32, name="y_ps%d" % t, tag="low%d" % t)
             nc.tensor.matmul_mx(
-                y_ps[:], lhsT=w1d[t].bitcast(FP8X4), lhsT_scale=w1sd[t],
+                y_ps[:], lhsT=w1d[:, t, :].bitcast(FP8X4), lhsT_scale=w1sd[t],
                 rhs=xg[:].bitcast(FP8X4), rhs_scale=xgs[:], start=True, stop=True,
             )
             nc.vector.tensor_copy(window[t][:, :S], y_ps[:])
 
         mb = [tile("mb%d" % t, [P, 2 * S], F32) for t in range(PACK)]
         for t in range(PACK):
-            for u in range(2):
-                nc.scalar.activation(
-                    mb[t][:, u * S : (u + 1) * S], window[t][:].indirect(n1_t[:, 16 * u : 16 * u + 16]), ACT.Copy
-                )
+            nc.scalar.activation(mb[t][:], window[t][:].indirect(n1_t[:]), ACT.Copy)
         y3 = [tile("y3_%d" % t, [P, S], F32) for t in range(PACK)]
         y4 = [tile("y4_%d" % t, [P, S], F32) for t in range(PACK)]
         for t in range(PACK):
@@ -176,27 +176,42 @@ def tile_picked_joingpairtrimgate_none_po_kernel(
                     rest[:, t, :], top34[t][:], gm_t[:, t : t + 1], yg[t][:], ALU.mult, ALU.subtract
                 )
 
-        h_ps = [psum.tile([P, S], F32, name="h_ps%d" % t) for t in range(PACK)]
-        for t in range(PACK):
-            nc.tensor.matmul_mx(
-                h_ps[t][:], lhsT=w2d[:, t, :].bitcast(FP8X4), lhsT_scale=w23sd[:, t, :],
-                rhs=zq[:].bitcast(FP8X4), rhs_scale=zs[:], start=True, stop=False,
-            )
+        h_ps = [
+            [psum.tile([P, HALF], F32, name="h_ps%d_%d" % (u, t), tag=("low%d", "high%d")[u] % t) for t in range(PACK)]
+            for u in range(2)
+        ]
         for u in range(2):
             cols = slice(u * HALF, (u + 1) * HALF)
-            z2_bf = tile("z2_bf%d" % u, [P, HALF * PACK], BF16)
-            nc.vector.tensor_tensor(woven(z2_bf[:]), planes(yg2[u][:]), planes(rest[:, :, cols]), ALU.subtract)
-            z2q = tile("z2q%d" % u, [P, HALF], U32)
-            z2s = tile("z2s%d" % u, [P, HALF], U8)
-            nc.vector.quantize_mx(z2q[:].bitcast(FP8X4), z2s[:], z2_bf[:])
             for t in range(PACK):
                 nc.tensor.matmul_mx(
-                    h_ps[t][:, cols], lhsT=w3d[:, t, :].bitcast(FP8X4), lhsT_scale=w23sd[4:, t, :],
-                    rhs=z2q[:].bitcast(FP8X4), rhs_scale=z2s[:], start=False, stop=(u == 1),
+                    h_ps[u][t][:], lhsT=w2d[:, t, :].bitcast(FP8X4), lhsT_scale=w23sd[:, t, :],
+                    rhs=zq[:, cols].bitcast(FP8X4), rhs_scale=zs[:, cols], start=True, stop=False,
+                )
+        for u in range(2):
+            cols = slice(u * HALF, (u + 1) * HALF)
+            pieces = u + 1
+            width = HALF // pieces
+            z2_bf = [tile("z2_bf%d_%d" % (u, v), [P, width * PACK], BF16) for v in range(pieces)]
+            z2q = tile("z2q%d" % u, [P, HALF], U32)
+            z2s = tile("z2s%d" % u, [P, HALF], U8)
+            for v in range(pieces):
+                part = slice(v * width, (v + 1) * width)
+                nc.vector.tensor_tensor(
+                    woven(z2_bf[v][:]), planes(yg2[u][:, :, part]), planes(rest[:, :, cols][:, :, part]), ALU.subtract
+                )
+            for v in range(pieces):
+                part = slice(v * width, (v + 1) * width)
+                nc.vector.quantize_mx(z2q[:, part].bitcast(FP8X4), z2s[:, part], z2_bf[v][:])
+            for t in range(PACK):
+                nc.tensor.matmul_mx(
+                    h_ps[u][t][:], lhsT=w3d[:, t, :].bitcast(FP8X4), lhsT_scale=w23sd[4:, t, :],
+                    rhs=z2q[:].bitcast(FP8X4), rhs_scale=z2s[:], start=False, stop=True,
                 )
 
         for t in range(PACK):
-            nc.vector.tensor_copy(window[t][:, :S], h_ps[t][:])
+            nc.scalar.copy(h_window[t][:, :HALF], h_ps[0][t][:])
+        for t in range(PACK):
+            nc.vector.tensor_copy(h_window[t][:, HALF:S], h_ps[1][t][:])
 
         oq = tile("oq", [P, S], U32)
         osc = tile("osc", [P, S], U8)
@@ -206,12 +221,17 @@ def tile_picked_joingpairtrimgate_none_po_kernel(
             gate = tile("gate%d" % u, [P, PACK, HALF], F32)
             res = tile("res%d" % u, [P, PACK, HALF], F32)
             for t in range(PACK):
-                nc.scalar.activation(gate[:, t, :], window[t][:].indirect(n5_t[:, 8 * u : 8 * u + 8]), ACT.Sigmoid)
-                nc.vector.tensor_tensor(res[:, t, :], gate[:, t, :], window[t][:, cols], ALU.mult)
+                nc.scalar.activation(gate[:, t, :], h_window[t][:].indirect(n5_t[:, 8 * u : 8 * u + 8]), ACT.Sigmoid)
+                nc.vector.tensor_tensor(res[:, t, :], gate[:, t, :], h_window[t][:, cols], ALU.mult)
             nc.sync.dma_start(out_rows[:, :, cols], res[:])
-            res_bf = tile("res_bf%d" % u, [P, HALF * PACK], BF16)
-            nc.vector.tensor_copy(woven(res_bf[:]), planes(res[:]))
-            nc.vector.quantize_mx(oq[:, cols].bitcast(FP8X4), osc[:, cols], res_bf[:])
+            pieces = u + 1
+            width = HALF // pieces
+            res_bf = [tile("res_bf%d_%d" % (u, v), [P, width * PACK], BF16) for v in range(pieces)]
+            for v in range(pieces):
+                nc.vector.tensor_copy(woven(res_bf[v][:]), planes(res[:, :, v * width : (v + 1) * width]))
+            for v in range(pieces):
+                part = slice(u * HALF + v * width, u * HALF + (v + 1) * width)
+                nc.vector.quantize_mx(oq[:, part].bitcast(FP8X4), osc[:, part], res_bf[v][:])
             nc.sync.dma_start(words_of(out_1)[:, cols], oq[:, cols].bitcast(I32))
         for q in range(4):
             queue = nc.scalar if q % 2 else nc.sync

@@ -60,10 +60,13 @@ def tile_picked_joingpairtrimgate_none_po_kernel(
                 dram[0, 4 * q : 4 * q + 4, :].bitcast(I32),
             )
 
-        def deal(dst, src, first=0, last=PACK):
+        def deal_words(dst, src):
             nc.vector.tensor_copy(
-                dst.rearrange("p t m -> p m t"), src.rearrange("p (m t) -> p m t", t=PACK)[:, :, first:last]
+                dst.rearrange("p t (a m) -> p a t m", m=4), src.rearrange("p (a m t) -> p a t m", m=4, t=PACK)
             )
+
+        def deal_scales(dst, src, first=0, last=PACK):
+            nc.vector.tensor_copy(dst, src.rearrange("p (m t) -> p t m", t=PACK)[:, first:last, :])
 
         xs = tile("xs", [P, T], U8)
         w1s = tile("w1s", [P, H], U8)
@@ -105,7 +108,7 @@ def tile_picked_joingpairtrimgate_none_po_kernel(
         n5_t = load_list("n5_t", n5)
 
         w1d = tile("w1d", [P, PACK, P], U32)
-        deal(w1d[:], w1w[:])
+        deal_words(w1d[:], w1w[:])
         xgs = tile("xgs", [P, S], U8)
         nc.vector.tensor_copy(xgs[:], xs[:].indirect(offs_t[:]))
         xg = tile("xg", [P, S], U32)
@@ -113,7 +116,7 @@ def tile_picked_joingpairtrimgate_none_po_kernel(
         w1sd = []
         for first, last in ((0, 1), (1, PACK)):
             dealt_scales = tile("w1sd%d" % first, [P, last - first, P], U8)
-            deal(dealt_scales[:], w1s[:], first, last)
+            deal_scales(dealt_scales[:], w1s[:], first, last)
             w1sd.extend(dealt_scales[:, t, :] for t in range(last - first))
 
         for t in range(PACK):
@@ -122,7 +125,10 @@ def tile_picked_joingpairtrimgate_none_po_kernel(
                 y_ps[:], lhsT=w1d[:, t, :].bitcast(FP8X4), lhsT_scale=w1sd[t],
                 rhs=xg[:].bitcast(FP8X4), rhs_scale=xgs[:], start=True, stop=True,
             )
-            nc.vector.tensor_copy(window[t][:, :S], y_ps[:])
+            if t == 0:
+                nc.scalar.copy(window[t][:, :S], y_ps[:])
+            else:
+                nc.vector.tensor_copy(window[t][:, :S], y_ps[:])
 
         mb = [tile("mb%d" % t, [P, 2 * S], F32) for t in range(PACK)]
         for t in range(PACK):
@@ -142,11 +148,11 @@ def tile_picked_joingpairtrimgate_none_po_kernel(
                 nc.scalar.activation(yg2[u][:, t, :], yg[t][:].indirect(n2_t[:, 8 * u : 8 * u + 8]), ACT.Copy)
 
         w2d = tile("w2d", [P, PACK, P], U32)
-        deal(w2d[:], w2w[:])
+        deal_words(w2d[:], w2w[:])
         w3d = tile("w3d", [P, PACK, P], U32)
-        deal(w3d[:], w3w[:])
+        deal_words(w3d[:], w3w[:])
         w23sd = tile("w23sd", [P, PACK, P], U8)
-        deal(w23sd[:], w23s[:])
+        deal_scales(w23sd[:], w23s[:])
 
         top = [tile("top%d" % t, [P, S], F32) for t in range(PACK)]
         gap = [tile("gap%d" % t, [P, S], F32) for t in range(PACK)]

@@ -157,13 +157,16 @@ def tile_picked_joingpairtrimgate_none_po_kernel(
         top = [tile("top%d" % t, [P, S], F32) for t in range(PACK)]
         gap = [tile("gap%d" % t, [P, S], F32) for t in range(PACK)]
         trimmed = tile("trimmed", [P, PACK, S], F32)
+        members = [tile("members%d" % t, [P, 2, S], F32) for t in range(PACK)]
         for pair in ((0, 1), (2, 3)):
             for t in pair:
-                nc.vector.tensor_tensor(top[t][:], mb[t][:, 0::2], window[t][:, :S], ALU.max)
+                nc.vector.tensor_copy(members[t][:].rearrange("p e j -> p j e"), mb[t][:].rearrange("p (j e) -> p j e", e=2))
             for t in pair:
-                nc.vector.tensor_tensor(gap[t][:], mb[t][:, 1::2], top[t][:], ALU.subtract)
+                nc.vector.tensor_tensor(top[t][:], members[t][:, 0, :], window[t][:, :S], ALU.max)
             for t in pair:
-                nc.vector.scalar_tensor_tensor(trimmed[:, t, :], gap[t][:], 0.0, mb[t][:, 0::2], ALU.min, ALU.add)
+                nc.vector.tensor_tensor(gap[t][:], members[t][:, 1, :], top[t][:], ALU.subtract)
+            for t in pair:
+                nc.vector.scalar_tensor_tensor(trimmed[:, t, :], gap[t][:], 0.0, members[t][:, 0, :], ALU.min, ALU.add)
         z_bf = tile("z_bf", [P, S * PACK], BF16)
         gn_wide = gn_t[:].rearrange("p (c t i) -> p c t i", c=1, i=1).to_broadcast([P, S // RUN, PACK, RUN])
         nc.vector.tensor_tensor(woven(z_bf[:]), planes(trimmed[:]), gn_wide, ALU.mult)

from contextlib import ExitStack

import concourse.mybir as mybir

F32 = mybir.dt.float32
BF16 = mybir.dt.bfloat16
I32 = mybir.dt.int32
U32 = mybir.dt.uint32
U16 = mybir.dt.uint16
U8 = mybir.dt.uint8
FP8X4 = mybir.dt.float8_e4m3fn_x4
ALU = mybir.AluOpType
ACT = mybir.ActivationFunctionType

P = 128
PACK = 4
T = 2048
S = 256
H = 512
HALF = S // 2
WINDOW = 2 * S
Y_WINDOW = 2 * S + 16
RUN = 2
FLOPS = 3 * 2 * 512 * 512 * 256


def words_of(dram):
    return dram[0].rearrange("p n t -> p (n t)").bitcast(I32)


def woven(ap):
    return ap.rearrange("p (c i t) -> p c t i", i=RUN, t=PACK)


def planes(ap):
    return ap.rearrange("p t (c i) -> p c t i", i=RUN)


def tile_picked_joingpairtrimgate_none_po_kernel(
    tc, x_words, x_scales, w1_words, w1_scales, gn, gm, w2_words, w2_scales, w3_words, w3_scales,
    offs, n1, n2, n3, n4, n5, out_0, out_1, out_2,
):
    nc = tc.nc
    with ExitStack() as ctx:
        lists = ctx.enter_context(tc.tile_pool(name="lists", bufs=1))
        sb = ctx.enter_context(tc.tile_pool(name="sb", bufs=1))
        psum = ctx.enter_context(tc.psum_pool(name="psum", bufs=1))

        def tile(name, shape, dtype):
            return sb.tile(shape, dtype, name=name, align_bytes=64)

        def load_list(name, dram):
            held = lists.tile(list(dram.shape), U16, name=name)
            nc.sync.dma_start(held[:], dram)
            return held

        def load_scale_rows(queue, plane, first, dram, q):
            queue.dma_start(
                plane[32 * q + first : 32 * q + first + 4, :].bitcast(I32),
                dram[0, 4 * q : 4 * q + 4, :].bitcast(I32),
            )

        def deal_words(dst, src):
            nc.vector.tensor_copy(
                dst.rearrange("p t (a m) -> p a t m", m=4), src.rearrange("p (a m t) -> p a t m", m=4, t=PACK)
            )

        def deal_scales(dst, src, first=0, last=PACK):
            nc.vector.tensor_copy(dst, src.rearrange("p (m t) -> p t m", t=PACK)[:, first:last, :])

        xs = tile("xs", [P, T], U8)
        w1s = tile("w1s", [P, H], U8)
        w23s = tile("w23s", [P, H], U8)
        nc.vector.memset(xs[:].bitcast(I32), 0)
        nc.vector.memset(w1s[:].bitcast(I32), 0)
        nc.vector.memset(w23s[:].bitcast(I32), 0)
        window = [tile("window%d" % t, [P, Y_WINDOW], F32) for t in range(PACK)]
        h_window = [tile("h_window%d" % t, [P, WINDOW], F32) for t in range(PACK)]
        for held in window + h_window:
            nc.vector.memset(held[:, S:], 0.0)

        offs_t = load_list("offs_t", offs)
        n1_t = load_list("n1_t", n1)
        w1w = tile("w1w", [P, H], U32)
        nc.sync.dma_start(w1w[:].bitcast(I32), words_of(w1_words))
        for q in range(4):
            load_scale_rows(nc.sync if q < 2 else nc.scalar, xs, 0, x_scales, q)
        warm = tile("warm", [P, 1], F32)
        nc.scalar.activation(warm[:], window[0][:, S : S + 1], ACT.Sigmoid)
        xw = tile("xw", [P, T], U32)
        nc.sync.dma_start(xw[:].bitcast(I32), words_of(x_words))
        for q in range(4):
            load_scale_rows(nc.sync, w1s, 0, w1_scales, q)
        w2w = tile("w2w", [P, H], U32)
        nc.sync.dma_start(w2w[:].bitcast(I32), words_of(w2_words))
        w3w = tile("w3w", [P, H], U32)
        nc.sync.dma_start(w3w[:].bitcast(I32), words_of(w3_words))
        for first, dram in ((0, w2_scales), (4, w3_scales)):
            for q in range(4):
                load_scale_rows(nc.sync, w23s, first, dram, q)
        gm_t = tile("gm_t", [P, PACK], F32)
        nc.gpsimd.dma_start(gm_t[:], gm.rearrange("(p t) o -> p (t o)", t=PACK))
        gn_t = tile("gn_t", [P, PACK], F32)
        nc.gpsimd.dma_start(gn_t[:], gn.rearrange("(p t) o -> p (t o)", t=PACK))
        n3_t = load_list("n3_t", n3)
        n4_t = load_list("n4_t", n4)
        n2_t = load_list("n2_t", n2)
        n5_t = load_list("n5_t", n5)

        w1d = tile("w1d", [P, PACK, P], U32)
        deal_words(w1d[:], w1w[:])
        xgs = tile("xgs", [P, S], U8)
        nc.vector.tensor_copy(xgs[:], xs[:].indirect(offs_t[:]))
        xg = tile("xg", [P, S], U32)
        nc.vector.tensor_copy(xg[:], xw[:].indirect(offs_t[:]))
        w1sd = []
        for first, last in ((0, 1), (1, PACK)):
            dealt_scales = tile("w1sd%d" % first, [P, last - first, P], U8)
            deal_scales(dealt_scales[:], w1s[:], first, last)
            w1sd.extend(dealt_scales[:, t, :] for t in range(last - first))

        for t in range(PACK):
            y_ps = psum.tile([P, S], F32, name="y_ps%d" % t, tag="low%d" % t)
            nc.tensor.matmul_mx(
                y_ps[:], lhsT=w1d[:, t, :].bitcast(FP8X4), lhsT_scale=w1sd[t],
                rhs=xg[:].bitcast(FP8X4), rhs_scale=xgs[:], start=True, stop=True,
            )
            if t == 0:
                nc.scalar.copy(window[t][:, :S], y_ps[:])
            else:
                nc.vector.tensor_copy(window[t][:, :S], y_ps[:])

        mb = [tile("mb%d" % t, [P, 2 * S], F32) for t in range(PACK)]
        for t in range(PACK):
            nc.scalar.activation(mb[t][:], window[t][:].indirect(n1_t[:]), ACT.Copy)
        y3 = [tile("y3_%d" % t, [P, S], F32) for t in range(PACK)]
        y4 = [tile("y4_%d" % t, [P, S], F32) for t in range(PACK)]
        for t in range(PACK):
            nc.scalar.activation(y3[t][:], window[t][:].indirect(n3_t[:]), ACT.Copy)
            nc.scalar.activation(y4[t][:], window[t][:].indirect(n4_t[:]), ACT.Copy)

        yg = [tile("yg%d" % t, [P, S], F32) for t in range(PACK)]
        for t in range(PACK):
            nc.vector.tensor_scalar(yg[t][:], window[t][:, :S], gm_t[:, t : t + 1], None, ALU.mult)
        yg2 = [tile("yg2_%d" % u, [P, PACK, HALF], F32) for u in range(2)]
        for u in range(2):
            for t in range(PACK):
                nc.scalar.activation(yg2[u][:, t, :], yg[t][:].indirect(n2_t[:, 8 * u : 8 * u + 8]), ACT.Copy)

        w2d = tile("w2d", [P, PACK, P], U32)
        deal_words(w2d[:], w2w[:])
        w3d = tile("w3d", [P, PACK, P], U32)
        deal_words(w3d[:], w3w[:])
        w23sd = tile("w23sd", [P, PACK, P], U8)
        deal_scales(w23sd[:], w23s[:])

        top = [tile("top%d" % t, [P, S], F32) for t in range(PACK)]
        gap = [tile("gap%d" % t, [P, S], F32) for t in range(PACK)]
        trimmed = tile("trimmed", [P, PACK, S], F32)
        members = [tile("members%d" % t, [P, 2, S], F32) for t in range(PACK)]
        for pair in ((0, 1), (2, 3)):
            for t in pair:
                nc.vector.tensor_copy(members[t][:].rearrange("p e j -> p j e"), mb[t][:].rearrange("p (j e) -> p j e", e=2))
            for t in pair:
                nc.vector.tensor_tensor(top[t][:], members[t][:, 0, :], window[t][:, :S], ALU.max)
            for t in pair:
                nc.vector.tensor_tensor(gap[t][:], members[t][:, 1, :], top[t][:], ALU.subtract)
            for t in pair:
                nc.vector.scalar_tensor_tensor(trimmed[:, t, :], gap[t][:], 0.0, members[t][:, 0, :], ALU.min, ALU.add)
        z_bf = tile("z_bf", [P, S * PACK], BF16)
        gn_wide = gn_t[:].rearrange("p (c t i) -> p c t i", c=1, i=1).to_broadcast([P, S // RUN, PACK, RUN])
        nc.vector.tensor_tensor(woven(z_bf[:]), planes(trimmed[:]), gn_wide, ALU.mult)

        top34 = [tile("top34_%d" % t, [P, S], F32) for t in range(PACK)]
        rest = tile("rest", [P, PACK, S], F32)
        zq = tile("zq", [P, S], U32)
        zs = tile("zs", [P, S], U8)
        for pair in ((0, 1), (2, 3)):
            for t in pair:
                nc.vector.tensor_tensor(top34[t][:], y3[t][:], y4[t][:], ALU.max)
            if pair[0] == 0:
                nc.vector.quantize_mx(zq[:].bitcast(FP8X4), zs[:], z_bf[:])
            for t in pair:
                nc.vector.scalar_tensor_tensor(
                    rest[:, t, :], top34[t][:], gm_t[:, t : t + 1], yg[t][:], ALU.mult, ALU.subtract
                )

        h_ps = [
            [psum.tile([P, HALF], F32, name="h_ps%d_%d" % (u, t), tag=("low%d", "high%d")[u] % t) for t in range(PACK)]
            for u in range(2)
        ]
        for u in range(2):
            cols = slice(u * HALF, (u + 1) * HALF)
            for t in range(PACK):
                nc.tensor.matmul_mx(
                    h_ps[u][t][:], lhsT=w2d[:, t, :].bitcast(FP8X4), lhsT_scale=w23sd[:, t, :],
                    rhs=zq[:, cols].bitcast(FP8X4), rhs_scale=zs[:, cols], start=True, stop=False,
                )
        for u in range(2):
            cols = slice(u * HALF, (u + 1) * HALF)
            pieces = u + 1
            width = HALF // pieces
            z2_bf = [tile("z2_bf%d_%d" % (u, v), [P, width * PACK], BF16) for v in range(pieces)]
            z2q = tile("z2q%d" % u, [P, HALF], U32)
            z2s = tile("z2s%d" % u, [P, HALF], U8)
            for v in range(pieces):
                part = slice(v * width, (v + 1) * width)
                nc.vector.tensor_tensor(
                    woven(z2_bf[v][:]), planes(yg2[u][:, :, part]), planes(rest[:, :, cols][:, :, part]), ALU.subtract
                )
            for v in range(pieces):
                part = slice(v * width, (v + 1) * width)
                nc.vector.quantize_mx(z2q[:, part].bitcast(FP8X4), z2s[:, part], z2_bf[v][:])
            for t in range(PACK):
                nc.tensor.matmul_mx(
                    h_ps[u][t][:], lhsT=w3d[:, t, :].bitcast(FP8X4), lhsT_scale=w23sd[4:, t, :],
                    rhs=z2q[:].bitcast(FP8X4), rhs_scale=z2s[:], start=False, stop=True,
                )

        for t in range(PACK):
            nc.scalar.copy(h_window[t][:, :HALF], h_ps[0][t][:])
        for t in range(PACK):
            nc.vector.tensor_copy(h_window[t][:, HALF:S], h_ps[1][t][:])

        oq = tile("oq", [P, S], U32)
        osc = tile("osc", [P, S], U8)
        out_rows = out_0.rearrange("(p t) j -> p t j", t=PACK)
        for u in range(2):
            cols = slice(u * HALF, (u + 1) * HALF)
            gate = tile("gate%d" % u, [P, PACK, HALF], F32)
            res = tile("res%d" % u, [P, PACK, HALF], F32)
            for t in range(PACK):
                nc.scalar.activation(gate[:, t, :], h_window[t][:].indirect(n5_t[:, 8 * u : 8 * u + 8]), ACT.Sigmoid)
                nc.vector.tensor_tensor(res[:, t, :], gate[:, t, :], h_window[t][:, cols], ALU.mult)
            nc.sync.dma_start(out_rows[:, :, cols], res[:])
            pieces = u + 1
            width = HALF // pieces
            res_bf = [tile("res_bf%d_%d" % (u, v), [P, width * PACK], BF16) for v in range(pieces)]
            for v in range(pieces):
                nc.vector.tensor_copy(woven(res_bf[v][:]), planes(res[:, :, v * width : (v + 1) * width]))
            for v in range(pieces):
                part = slice(u * HALF + v * width, u * HALF + (v + 1) * width)
                nc.vector.quantize_mx(oq[:, part].bitcast(FP8X4), osc[:, part], res_bf[v][:])
            nc.sync.dma_start(words_of(out_1)[:, cols], oq[:, cols].bitcast(I32))
        for q in range(4):
            queue = nc.scalar if q % 2 else nc.sync
            queue.dma_start(out_2[0, 4 * q : 4 * q + 4, :].bitcast(I32), osc[32 * q : 32 * q + 4, :].bitcast(I32))
